import numpy as np
import ml_dtypes


def mxq(x, axis, fmt="e4m3"):
    dtype, down = {"e4m3": (ml_dtypes.float8_e4m3fn, 7), "e5m2": (ml_dtypes.float8_e5m2, 14)}[fmt]
    v = np.moveaxis(np.asarray(x, np.float32).astype(ml_dtypes.bfloat16).astype(np.float64), axis, -1)
    blocks = v.reshape(v.shape[:-1] + (-1, 32))
    amax = np.abs(blocks).max(-1, keepdims=True)
    byte = np.maximum(np.where(amax > 0, np.frexp(amax)[1] - 1 + 127, 0) - down, 1)
    scale = np.exp2(byte - 127.0)
    codes = (blocks / scale).astype(np.float32).astype(dtype).astype(np.float64)
    return np.moveaxis((codes * scale).reshape(v.shape), -1, axis)


WIDE = False


def mx_kscale(k):
    if not WIDE:
        return np.ones(k)
    levels = np.array([10, -10, 5, -5, 0])
    if k % 512:
        return np.exp2(np.random.permutation(np.resize(levels, k // 32))).repeat(32)
    a = np.empty((k // 512, 16))
    for p in range(k // 512):
        a[p, :8] = np.random.permutation(np.resize(levels, 8))
        for g in range(8):
            far = levels[np.abs(levels - a[p, g]) >= 10]
            a[p, g + 8] = far[np.random.randint(len(far))]
    return np.exp2(a.ravel()).repeat(32)


def f64(x):
    return np.asarray(x).astype(np.float64)


def striped(idx):
    return np.tile(idx.reshape(-1, 16).T, (8, 1)).astype(np.uint16)


def unstriped(offs):
    return offs[:16].T.reshape(-1).astype(np.int64)


def striped8(idx):
    return np.concatenate([x.reshape(-1, 16).T for x in idx]).astype(np.uint16)


def runs(offs, k):
    lists = np.stack([offs[16 * r : 16 * r + 16].T.reshape(-1) for r in range(8)]).astype(np.int64)
    return lists[np.arange(k) % 512 // 64]


def pack_weight(w):
    k, n = w.shape
    w = f64(np.asarray(w, np.float32).astype(ml_dtypes.bfloat16)).reshape(k // 32, 32, n)
    amax = np.abs(w).max(1)
    byte = np.clip(np.where(amax > 0, np.frexp(amax)[1] - 1 + 127 - 7, 1), 1, 254)
    scaled = (w * np.exp2(127.0 - byte)[:, None, :]).reshape(k, n).astype(np.float32)
    words = np.ascontiguousarray(scaled.reshape(k // 512, 128, 4, n).transpose(0, 1, 3, 2)).astype(ml_dtypes.float8_e4m3fn).view(np.uint8)
    return words, np.ascontiguousarray(byte.astype(np.uint8).reshape(k // 512, 16, n))


def unpack_weight(words, scales):
    g, p, n, _ = words.shape
    vals = np.ascontiguousarray(words).view(ml_dtypes.float8_e4m3fn).astype(np.float64) * np.repeat(np.exp2(scales.astype(np.float64) - 127.0), 8, axis=1)[..., None]
    return vals.transpose(0, 1, 3, 2).reshape(g * 512, n)

def planes(y):
    n, m = y.shape
    v = y.astype(np.float32).astype(ml_dtypes.bfloat16).astype(np.float64).reshape(n // 32, 32, m)
    top = np.abs(v).max(1)
    byte = np.clip(np.where(top > 0, np.frexp(top)[1] - 1 + 127 - 7, 1), 1, 254)
    codes = (v * np.exp2(127.0 - byte)[:, None, :]).reshape(n, m).astype(np.float32).astype(ml_dtypes.float8_e4m3fn).view(np.uint8)
    words = codes.reshape(n // 512, 128, 4, m).transpose(0, 1, 3, 2)
    return np.ascontiguousarray(words), np.ascontiguousarray(byte.astype(np.uint8).reshape(n // 512, 16, m))


K, T, S, N, H = 512, 2048, 512, 512, 512


def setup_inputs():
    n = np.random.standard_normal
    s = mx_kscale(K)[:, None]
    u = mx_kscale(H)
    packed_xT = pack_weight(n((K, T)) * s)
    packed_w3 = pack_weight(n((H, N)) / np.sqrt(H) / u[:, None])
    return {
        "x_words": packed_xT[0],
        "x_scales": packed_xT[1],
        "w1": (n((K, H)) / np.sqrt(K) / s * u).astype(np.float32),
        "w2": (n((H, H)) / np.sqrt(H) / u[:, None] * u).astype(np.float32),
        "w3_words": packed_w3[0],
        "w3_scales": packed_w3[1],
        "res": n((N, S)).astype(np.float32),
        "offs": striped(np.random.permutation(T)[:S]),
        "n1": striped8(np.stack([np.random.permutation(S) for _ in range(8)])),
        "n2": striped8(np.stack([np.random.permutation(S) for _ in range(8)])),
    }


def reference(x_words, x_scales, w1, w2, w3_words, w3_scales, res, offs, n1, n2):
    xq = unpack_weight(x_words, x_scales)[:, unstriped(offs)]
    y = mxq(f64(w1), 0, "e4m3").T @ xq
    z = y[np.arange(H)[:, None], runs(n1, H)] + 0.5 * (y[np.arange(H)[:, None], runs(n2, H)])
    h = mxq(f64(w2), 0, "e4m3").T @ mxq(z, 0, "e4m3")
    z2 = np.maximum(h, h[np.arange(H)[:, None], runs(n1, H)]) - (np.minimum(h[np.arange(H)[:, None], runs(n2, H)], y))
    out_0 = f64(res) + (unpack_weight(w3_words, w3_scales).T @ mxq(z2, 0, "e4m3"))
    return (out_0,) + planes(out_0)

@@ -1,0 +1,242 @@
+from contextlib import ExitStack
+
+import concourse.mybir as mybir
+
+F32 = mybir.dt.float32
+BF16 = mybir.dt.bfloat16
+I32 = mybir.dt.int32
+U32 = mybir.dt.uint32
+U16 = mybir.dt.uint16
+U8 = mybir.dt.uint8
+FP8X4 = mybir.dt.float8_e4m3fn_x4
+ALU = mybir.AluOpType
+COPY = mybir.ActivationFunctionType.Copy
+
+P = 128
+PACK = 4
+T = 2048
+S = 512
+HALF = S // 2
+FLOPS = 3 * 2 * 512 * 512 * 512
+SLICES = ((0, 256), (256, 128), (384, 128))
+W1_SPLIT = 84
+
+
+def tile_picked_upenv_none_po_kernel(
+    tc, x_words, x_scales, w1, w2, w3_words, w3_scales, res, offs, n1, n2, out_0, out_1, out_2
+):
+    nc = tc.nc
+    with ExitStack() as ctx:
+        keep = ctx.enter_context(tc.tile_pool(name="keep", bufs=1))
+        psum = ctx.enter_context(tc.psum_pool(name="psum", bufs=1))
+
+        def sb(name, shape, dtype, tag=None):
+            return keep.tile(shape, dtype, name=name, tag=tag or name, align_bytes=64)
+
+        offs_sb = keep.tile([P, S // 16], U16, name="offs_sb")
+        n1_sb = keep.tile([P, S // 16], U16, name="n1_sb")
+        n2_sb = keep.tile([P, S // 16], U16, name="n2_sb")
+        x_word_table = sb("x_word_table", [P, T], U32)
+        x_scale_table = sb("x_scale_table", [P, T], U8, tag="scale_rows")
+        w1_raw = sb("w1_raw", [P, PACK, S], F32, tag="staged")
+
+        nc.gpsimd.memset(x_scale_table[:].bitcast(I32), 0)
+        for q in range(4):
+            nc.scalar.dma_start(
+                x_scale_table[32 * q : 32 * q + 4, :].bitcast(I32), x_scales[0, 4 * q : 4 * q + 4, :].bitcast(I32)
+            )
+        nc.sync.dma_start(w1_raw[:], w1.rearrange("(p j) c -> p j c", j=PACK))
+        nc.sync.dma_start(offs_sb[:], offs)
+        nc.sync.dma_start(x_word_table[:].bitcast(I32), x_words[0].rearrange("p n t -> p (n t)").bitcast(I32))
+        nc.sync.dma_start(n1_sb[:], n1)
+        nc.sync.dma_start(n2_sb[:], n2)
+
+        def dealt_views(grouped, raw, m0, m1):
+            dst = grouped[:].rearrange("p (t m j) -> p m j t", t=PACK, j=PACK)[:, m0:m1]
+            src = raw[:].rearrange("p j (m t) -> p m j t", t=PACK)[:, m0:m1]
+            return dst, src
+
+        def quantize(words, scales, grouped, c0, n):
+            nc.vector.quantize_mx(
+                out=words[:, c0 : c0 + n].bitcast(FP8X4), scales=scales[:, c0 : c0 + n], in_=grouped
+            )
+
+        def product(out, w_words, w_scales, t, a_words, a_scales, c0, n):
+            nc.tensor.matmul_mx(
+                out=out,
+                lhsT=w_words[:, P * t : P * (t + 1)].bitcast(FP8X4),
+                lhsT_scale=w_scales[:, P * t : P * (t + 1)],
+                rhs=a_words[:, c0 : c0 + n].bitcast(FP8X4),
+                rhs_scale=a_scales[:, c0 : c0 + n],
+                start=True,
+                stop=True,
+            )
+
+        def woven(grouped, run):
+            return grouped[:].rearrange("p (c i t) -> p c t i", i=run, t=PACK)
+
+        def planar(planes, run):
+            return planes[:].rearrange("p t (c i) -> p c t i", i=run)
+
+        x_scale_pick = sb("x_scale_pick", [P, S], U8)
+        nc.vector.tensor_copy(x_scale_pick[:], x_scale_table[:].indirect(offs_sb[:]))
+        w1_grouped = sb("w1_grouped", [P, PACK * S], BF16, tag="w1_then_w3")
+        dst, src = dealt_views(w1_grouped, w1_raw, 0, W1_SPLIT)
+        nc.vector.tensor_copy(dst, src)
+        dst, src = dealt_views(w1_grouped, w1_raw, W1_SPLIT, P)
+        nc.scalar.activation(dst, src, COPY)
+        w1_words = sb("w1_words", [P, S], U32)
+        w1_scales = sb("w1_scales", [P, S], U8)
+        quantize(w1_words, w1_scales, w1_grouped[:], 0, S)
+        w2_raw = sb("w2_raw", [P, PACK, S], F32, tag="staged")
+        nc.sync.dma_start(w2_raw[:], w2.rearrange("(p j) c -> p j c", j=PACK))
+        w3_word_raw = sb("w3_word_raw", [P, S], U32, tag="w1_then_w3")
+        nc.sync.dma_start(w3_word_raw[:].bitcast(I32), w3_words[0].rearrange("p n t -> p (n t)").bitcast(I32))
+        w3_scale_raw = sb("w3_scale_raw", [P, S], U8, tag="scale_rows")
+        nc.gpsimd.memset(w3_scale_raw[:].bitcast(I32), 0)
+        for q in range(4):
+            nc.sync.dma_start(
+                w3_scale_raw[32 * q : 32 * q + 4, :].bitcast(I32), w3_scales[0, 4 * q : 4 * q + 4, :].bitcast(I32)
+            )
+        x_word_pick = [sb(f"x_word_pick{b}", [P, HALF], U32) for b in range(2)]
+        for b in range(2):
+            nc.vector.tensor_copy(x_word_pick[b][:], x_word_table[:].indirect(offs_sb[:, 16 * b : 16 * (b + 1)]))
+
+        def bank(tag, shape, name):
+            return psum.tile(shape, F32, name=name, tag=tag)
+
+        y_bank = [[bank(f"y{b}{u}", [P, 2, HALF], f"y_bank{b}{u}") for u in range(2)] for b in range(2)]
+        h_bank = [[bank(f"h{b}{u}", [P, 2, HALF], f"h_bank{b}{u}") for u in range(2)] for b in range(2)]
+        y_rows = [sb(f"y_rows{t}", [P, S], F32) for t in range(PACK)]
+        h_rows = [sb(f"h_rows{t}", [P, S], F32) for t in range(PACK)]
+
+        for u in range(2):
+            for b in range(2):
+                for e in range(2):
+                    nc.tensor.matmul_mx(
+                        out=y_bank[b][u][:, e, :],
+                        lhsT=w1_words[:, P * (2 * u + e) : P * (2 * u + e + 1)].bitcast(FP8X4),
+                        lhsT_scale=w1_scales[:, P * (2 * u + e) : P * (2 * u + e + 1)],
+                        rhs=x_word_pick[b][:].bitcast(FP8X4),
+                        rhs_scale=x_scale_pick[:, HALF * b : HALF * (b + 1)],
+                        start=True,
+                        stop=True,
+                    )
+        for u in range(2):
+            for e in range(2):
+                t = 2 * u + e
+                nc.scalar.activation(y_rows[t][:, 0:HALF], y_bank[0][u][:, e, :], COPY)
+                nc.vector.tensor_copy(y_rows[t][:, HALF:S], y_bank[1][u][:, e, :])
+
+        def fetch(on_vector, out, rows, index, c0, n, scale=1.0):
+            picked = rows[:].indirect(index[:, c0 // 16 : (c0 + n) // 16])
+            if on_vector:
+                nc.vector.tensor_copy(out, picked)
+            else:
+                nc.scalar.activation(out, picked, COPY, scale=scale)
+
+        w2_grouped = sb("w2_grouped", [P, PACK * S], BF16)
+        w2_words = sb("w2_words", [P, S], U32)
+        w2_scales = sb("w2_scales", [P, S], U8)
+        z_words = sb("z_words", [P, S], U32)
+        z_scales = sb("z_scales", [P, S], U8)
+        y_at_n1 = [sb(f"y_at_n1_{c0}", [P, PACK, n], F32) for c0, n in SLICES]
+        y_at_n2 = [sb(f"y_at_n2_{c0}", [P, PACK, n], F32) for c0, n in SLICES]
+        for s, (c0, n) in enumerate(SLICES):
+            for t in range(PACK):
+                fetch(False, y_at_n2[s][:, t, :], y_rows[t], n2_sb, c0, n, scale=0.5)
+                fetch(t < 2, y_at_n1[s][:, t, :], y_rows[t], n1_sb, c0, n)
+            if s == 0:
+                dst, src = dealt_views(w2_grouped, w2_raw, 0, P)
+                nc.vector.tensor_copy(dst, src)
+                quantize(w2_words, w2_scales, w2_grouped[:], 0, S)
+        res_sb = sb("res_sb", [P, PACK, S], F32, tag="staged")
+        nc.sync.dma_start(res_sb[:], res.rearrange("(p t) j -> p t j", t=PACK))
+        for s, (c0, n) in enumerate(SLICES):
+            z_grouped = sb(f"z_grouped{c0}", [P, PACK * n], BF16)
+            nc.vector.tensor_tensor(woven(z_grouped, 2), planar(y_at_n1[s], 2), planar(y_at_n2[s], 2), ALU.add)
+            quantize(z_words, z_scales, z_grouped[:], c0, n)
+            b, o = divmod(c0, HALF)
+            for t in range(PACK):
+                product(h_bank[b][t // 2][:, t % 2, o : o + n], w2_words, w2_scales, t, z_words, z_scales, c0, n)
+        for t in range(PACK):
+            nc.scalar.activation(h_rows[t][:, 0:HALF], h_bank[0][t // 2][:, t % 2, :], COPY)
+        w3_word_dealt = sb("w3_word_dealt", [P, S], U32)
+        w3_scale_dealt = sb("w3_scale_dealt", [P, S], U8)
+        nc.scalar.copy(
+            w3_word_dealt[:].rearrange("p (t m) -> p m t", t=PACK), w3_word_raw[:].rearrange("p (m t) -> p m t", t=PACK)
+        )
+        nc.vector.tensor_copy(
+            w3_scale_dealt[:].rearrange("p (t m) -> p m t", t=PACK), w3_scale_raw[:].rearrange("p (m t) -> p m t", t=PACK)
+        )
+        for t in range(PACK):
+            if t < 2:
+                nc.scalar.activation(h_rows[t][:, HALF:S], h_bank[1][t // 2][:, t % 2, :], COPY)
+            else:
+                nc.vector.tensor_copy(h_rows[t][:, HALF:S], h_bank[1][t // 2][:, t % 2, :])
+
+        z2_words = sb("z2_words", [P, S], U32)
+        z2_scales = sb("z2_scales", [P, S], U8)
+        out_words = sb("out_words", [P, S], U32)
+        out_scales = sb("out_scales", [P, S], U8)
+        out_rows = out_0.rearrange("(p t) j -> p t j", t=PACK)
+        out_word_rows = out_1[0].rearrange("p n t -> p (n t)").bitcast(I32)
+        out_tags = (("y00", "y01"), ("h00",), ("h01",))
+        result = [sb(f"result{c0}", [P, PACK, n], F32) for c0, n in SLICES]
+
+        def envelope(s):
+            c0, n = SLICES[s]
+            b, o = divmod(c0, HALF)
+            h_at_n1 = sb(f"h_at_n1_{c0}", [P, PACK, n], F32)
+            h_at_n2 = sb(f"h_at_n2_{c0}", [P, PACK, n], F32)
+            larger = sb(f"larger{c0}", [P, PACK, n], F32)
+            smaller = sb(f"smaller{c0}", [P, PACK, n], F32)
+            for u in range(2):
+                pair = slice(2 * u, 2 * u + 2)
+                for t in (2 * u, 2 * u + 1):
+                    fetch(s == 0 and t >= 1, h_at_n1[:, t, :], h_rows[t], n1_sb, c0, n)
+                for t in (2 * u, 2 * u + 1):
+                    fetch(False, h_at_n2[:, t, :], h_rows[t], n2_sb, c0, n)
+            for u in range(2):
+                pair = slice(2 * u, 2 * u + 2)
+                nc.vector.tensor_tensor(larger[:, pair, :], h_bank[b][u][:, :, o : o + n], h_at_n1[:, pair, :], ALU.max)
+                nc.vector.tensor_tensor(smaller[:, pair, :], y_bank[b][u][:, :, o : o + n], h_at_n2[:, pair, :], ALU.min)
+            z2_grouped = sb(f"z2_grouped{c0}", [P, PACK * n], BF16)
+            nc.vector.tensor_tensor(woven(z2_grouped, 2), planar(larger, 2), planar(smaller, 2), ALU.subtract)
+            quantize(z2_words, z2_scales, z2_grouped[:], c0, n)
+
+        def third_product(s):
+            c0, n = SLICES[s]
+            per_bank = PACK // len(out_tags[s])
+            for u, tag in enumerate(out_tags[s]):
+                acc = bank(tag, [P, per_bank, n], f"out_bank{c0}_{u}")
+                for e in range(per_bank):
+                    product(acc[:, e, :], w3_word_dealt, w3_scale_dealt, per_bank * u + e, z2_words, z2_scales, c0, n)
+                rows = slice(per_bank * u, per_bank * (u + 1))
+                nc.vector.tensor_tensor(result[s][:, rows, :], acc[:], res_sb[:, rows, c0 : c0 + n], ALU.add)
+            nc.sync.dma_start(out_rows[:, :, c0 : c0 + n], result[s][:])
+
+        def hand_on(s, on_vector):
+            c0, n = SLICES[s]
+            out_grouped = sb(f"out_grouped{c0}", [P, PACK * n], BF16)
+            if on_vector:
+                nc.vector.tensor_copy(woven(out_grouped, 4), planar(result[s], 4))
+            else:
+                nc.scalar.activation(woven(out_grouped, 4), planar(result[s], 4), COPY)
+            quantize(out_words, out_scales, out_grouped[:], c0, n)
+            nc.sync.dma_start(out_word_rows[:, c0 : c0 + n], out_words[:, c0 : c0 + n].bitcast(I32))
+
+        envelope(0)
+        third_product(0)
+        envelope(1)
+        third_product(1)
+        envelope(2)
+        hand_on(0, False)
+        hand_on(1, False)
+        third_product(2)
+        hand_on(2, True)
+        for q in range(4):
+            queue = nc.scalar if q % 2 else nc.sync
+            queue.dma_start(
+                out_2[0, 4 * q : 4 * q + 4, :].bitcast(I32), out_scales[32 * q : 32 * q + 4, :].bitcast(I32)
+            )

@@ -17,9 +17,16 @@ PACK = 4
 T = 2048
 S = 512
 HALF = S // 2
-FLOPS = 3 * 2 * 512 * 512 * 512
+QUADRANTS = 4
+PER_LIST_COLUMN = 16
+WEAVE_RUN = 4
+FLOPS = 3 * 2 * S * S * S
+
 SLICES = ((0, 256), (256, 128), (384, 128))
-W1_SPLIT = 84
+LAST = len(SLICES) - 1
+Y_TILES_SHARED = 2
+Z_SLICE_ON_SCALAR = 1
+H_GATHERS_ON_VECTOR = 3
 
 
 def tile_picked_upenv_none_po_kernel(
@@ -28,37 +35,43 @@ def tile_picked_upenv_none_po_kernel(
     nc = tc.nc
     with ExitStack() as ctx:
         keep = ctx.enter_context(tc.tile_pool(name="keep", bufs=1))
+        shared = ctx.enter_context(tc.tile_pool(name="shared", bufs=1))
         psum = ctx.enter_context(tc.psum_pool(name="psum", bufs=1))
 
         def sb(name, shape, dtype, tag=None):
             return keep.tile(shape, dtype, name=name, tag=tag or name, align_bytes=64)
 
-        offs_sb = keep.tile([P, S // 16], U16, name="offs_sb")
-        n1_sb = keep.tile([P, S // 16], U16, name="n1_sb")
-        n2_sb = keep.tile([P, S // 16], U16, name="n2_sb")
-        x_word_table = sb("x_word_table", [P, T], U32)
-        x_scale_table = sb("x_scale_table", [P, T], U8, tag="scale_rows")
-        w1_raw = sb("w1_raw", [P, PACK, S], F32, tag="staged")
+        def bank(name, shape, tag):
+            return psum.tile(shape, F32, name=name, tag=tag)
 
-        nc.gpsimd.memset(x_scale_table[:].bitcast(I32), 0)
-        for q in range(4):
-            nc.scalar.dma_start(
-                x_scale_table[32 * q : 32 * q + 4, :].bitcast(I32), x_scales[0, 4 * q : 4 * q + 4, :].bitcast(I32)
-            )
-        nc.sync.dma_start(w1_raw[:], w1.rearrange("(p j) c -> p j c", j=PACK))
-        nc.sync.dma_start(offs_sb[:], offs)
-        nc.sync.dma_start(x_word_table[:].bitcast(I32), x_words[0].rearrange("p n t -> p (n t)").bitcast(I32))
-        nc.sync.dma_start(n1_sb[:], n1)
-        nc.sync.dma_start(n2_sb[:], n2)
+        def copy(on_vector, dst, src):
+            if on_vector:
+                nc.vector.tensor_copy(dst, src)
+            else:
+                nc.scalar.activation(dst, src, COPY)
 
-        def dealt_views(grouped, raw, m0, m1):
-            dst = grouped[:].rearrange("p (t m j) -> p m j t", t=PACK, j=PACK)[:, m0:m1]
-            src = raw[:].rearrange("p j (m t) -> p m j t", t=PACK)[:, m0:m1]
-            return dst, src
+        def word_rows(packed):
+            return packed[0].rearrange("p n t -> p (n t)").bitcast(I32)
+
+        def load_scale_rows(queue, tile, scales):
+            nc.gpsimd.memset(tile[:].bitcast(I32), 0)
+            for q in range(QUADRANTS):
+                queue.dma_start(tile[32 * q : 32 * q + 4, :].bitcast(I32), scales[0, 4 * q : 4 * q + 4, :].bitcast(I32))
+
+        def deal_pair(on_vector, grouped, raw, pair):
+            dst = grouped.rearrange("p (t m j) -> p m j t", t=2, j=PACK)
+            src = raw[:].rearrange("p j (m t) -> p m j t", t=PACK)[:, :, :, 2 * pair : 2 * pair + 2]
+            copy(on_vector, dst, src)
+
+        def woven(grouped):
+            return grouped[:].rearrange("p (c i t) -> p c t i", i=WEAVE_RUN, t=PACK)
+
+        def planar(row_tiles):
+            return row_tiles[:].rearrange("p t (c i) -> p c t i", i=WEAVE_RUN)
 
         def quantize(words, scales, grouped, c0, n):
             nc.vector.quantize_mx(
-                out=words[:, c0 : c0 + n].bitcast(FP8X4), scales=scales[:, c0 : c0 + n], in_=grouped
+                out=words[:, c0 : c0 + n].bitcast(FP8X4), scales=scales[:, c0 : c0 + n], in_=grouped[:]
             )
 
         def product(out, w_words, w_scales, t, a_words, a_scales, c0, n):
@@ -72,116 +85,107 @@ def tile_picked_upenv_none_po_kernel(
                 stop=True,
             )
 
-        def woven(grouped, run):
-            return grouped[:].rearrange("p (c i t) -> p c t i", i=run, t=PACK)
+        def looked_up(rows, index, c0, n):
+            return rows[:].indirect(index[:, c0 // PER_LIST_COLUMN : (c0 + n) // PER_LIST_COLUMN])
 
-        def planar(planes, run):
-            return planes[:].rearrange("p t (c i) -> p c t i", i=run)
+        offs_sb = keep.tile([P, S // PER_LIST_COLUMN], U16, name="offs_sb")
+        n1_sb = keep.tile([P, S // PER_LIST_COLUMN], U16, name="n1_sb")
+        n2_sb = keep.tile([P, S // PER_LIST_COLUMN], U16, name="n2_sb")
+        x_word_table = shared.tile([P, T], U32, name="x_word_table", offset=0, align_bytes=64)
+        x_scale_table = sb("x_scale_table", [P, T], U8)
+        w1_raw = sb("w1_raw", [P, PACK, S], F32, tag="w1_raw_then_w3_words")
+        nc.sync.dma_start(offs_sb[:], offs)
+        load_scale_rows(nc.scalar, x_scale_table, x_scales)
+        nc.sync.dma_start(x_word_table[:].bitcast(I32), word_rows(x_words))
+        nc.sync.dma_start(w1_raw[:], w1.rearrange("(p j) c -> p j c", j=PACK))
+        nc.sync.dma_start(n1_sb[:], n1)
+        nc.sync.dma_start(n2_sb[:], n2)
 
-        x_scale_pick = sb("x_scale_pick", [P, S], U8)
+        x_word_pick = sb("x_word_pick", [P, S], U32)
+        nc.vector.tensor_copy(x_word_pick[:], x_word_table[:].indirect(offs_sb[:]))
+        x_scale_pick = shared.tile([P, S], U8, name="x_scale_pick", offset=0, align_bytes=64)
         nc.vector.tensor_copy(x_scale_pick[:], x_scale_table[:].indirect(offs_sb[:]))
-        w1_grouped = sb("w1_grouped", [P, PACK * S], BF16, tag="w1_then_w3")
-        dst, src = dealt_views(w1_grouped, w1_raw, 0, W1_SPLIT)
-        nc.vector.tensor_copy(dst, src)
-        dst, src = dealt_views(w1_grouped, w1_raw, W1_SPLIT, P)
-        nc.scalar.activation(dst, src, COPY)
+        w2_raw = shared.tile([P, PACK, S], F32, name="w2_raw", offset=S, align_bytes=64)
+        nc.sync.dma_start(w2_raw[:], w2.rearrange("(p j) c -> p j c", j=PACK))
+
         w1_words = sb("w1_words", [P, S], U32)
         w1_scales = sb("w1_scales", [P, S], U8)
-        quantize(w1_words, w1_scales, w1_grouped[:], 0, S)
-        w2_raw = sb("w2_raw", [P, PACK, S], F32, tag="staged")
-        nc.sync.dma_start(w2_raw[:], w2.rearrange("(p j) c -> p j c", j=PACK))
-        w3_word_raw = sb("w3_word_raw", [P, S], U32, tag="w1_then_w3")
-        nc.sync.dma_start(w3_word_raw[:].bitcast(I32), w3_words[0].rearrange("p n t -> p (n t)").bitcast(I32))
-        w3_scale_raw = sb("w3_scale_raw", [P, S], U8, tag="scale_rows")
-        nc.gpsimd.memset(w3_scale_raw[:].bitcast(I32), 0)
-        for q in range(4):
-            nc.sync.dma_start(
-                w3_scale_raw[32 * q : 32 * q + 4, :].bitcast(I32), w3_scales[0, 4 * q : 4 * q + 4, :].bitcast(I32)
-            )
-        x_word_pick = [sb(f"x_word_pick{b}", [P, HALF], U32) for b in range(2)]
-        for b in range(2):
-            nc.vector.tensor_copy(x_word_pick[b][:], x_word_table[:].indirect(offs_sb[:, 16 * b : 16 * (b + 1)]))
+        w1_grouped = [sb(f"w1_grouped{pair}", [P, 2 * S], BF16) for pair in range(2)]
+        for pair in range(2):
+            deal_pair(pair == 0, w1_grouped[pair][:], w1_raw, pair)
+            quantize(w1_words, w1_scales, w1_grouped[pair], HALF * pair, HALF)
+        w3_word_raw = sb("w3_word_raw", [P, S], U32, tag="w1_raw_then_w3_words")
+        nc.sync.dma_start(w3_word_raw[:].bitcast(I32), word_rows(w3_words))
+        w3_scale_raw = sb("w3_scale_raw", [P, S], U8, tag="w1_grouped0")
+        load_scale_rows(nc.sync, w3_scale_raw, w3_scales)
 
-        def bank(tag, shape, name):
-            return psum.tile(shape, F32, name=name, tag=tag)
-
-        y_bank = [[bank(f"y{b}{u}", [P, 2, HALF], f"y_bank{b}{u}") for u in range(2)] for b in range(2)]
-        h_bank = [[bank(f"h{b}{u}", [P, 2, HALF], f"h_bank{b}{u}") for u in range(2)] for b in range(2)]
+        y_bank = [[bank(f"y_bank{b}{u}", [P, 2, HALF], f"y{b}{u}") for u in range(2)] for b in range(2)]
+        h_bank = [[bank(f"h_bank{b}{u}", [P, 2, HALF], f"h{b}{u}") for u in range(2)] for b in range(2)]
         y_rows = [sb(f"y_rows{t}", [P, S], F32) for t in range(PACK)]
         h_rows = [sb(f"h_rows{t}", [P, S], F32) for t in range(PACK)]
 
-        for u in range(2):
+        for t in range(PACK):
             for b in range(2):
-                for e in range(2):
-                    nc.tensor.matmul_mx(
-                        out=y_bank[b][u][:, e, :],
-                        lhsT=w1_words[:, P * (2 * u + e) : P * (2 * u + e + 1)].bitcast(FP8X4),
-                        lhsT_scale=w1_scales[:, P * (2 * u + e) : P * (2 * u + e + 1)],
-                        rhs=x_word_pick[b][:].bitcast(FP8X4),
-                        rhs_scale=x_scale_pick[:, HALF * b : HALF * (b + 1)],
-                        start=True,
-                        stop=True,
-                    )
-        for u in range(2):
-            for e in range(2):
-                t = 2 * u + e
-                nc.scalar.activation(y_rows[t][:, 0:HALF], y_bank[0][u][:, e, :], COPY)
-                nc.vector.tensor_copy(y_rows[t][:, HALF:S], y_bank[1][u][:, e, :])
-
-        def fetch(on_vector, out, rows, index, c0, n, scale=1.0):
-            picked = rows[:].indirect(index[:, c0 // 16 : (c0 + n) // 16])
-            if on_vector:
-                nc.vector.tensor_copy(out, picked)
-            else:
-                nc.scalar.activation(out, picked, COPY, scale=scale)
+                product(y_bank[b][t % 2][:, t // 2, :], w1_words, w1_scales, t, x_word_pick, x_scale_pick, HALF * b, HALF)
+            for b in range(2):
+                on_vector = b == 1 and t < Y_TILES_SHARED
+                copy(on_vector, y_rows[t][:, HALF * b : HALF * (b + 1)], y_bank[b][t % 2][:, t // 2, :])
 
         w2_grouped = sb("w2_grouped", [P, PACK * S], BF16)
         w2_words = sb("w2_words", [P, S], U32)
         w2_scales = sb("w2_scales", [P, S], U8)
         z_words = sb("z_words", [P, S], U32)
         z_scales = sb("z_scales", [P, S], U8)
-        y_at_n1 = [sb(f"y_at_n1_{c0}", [P, PACK, n], F32) for c0, n in SLICES]
-        y_at_n2 = [sb(f"y_at_n2_{c0}", [P, PACK, n], F32) for c0, n in SLICES]
-        for s, (c0, n) in enumerate(SLICES):
-            for t in range(PACK):
-                fetch(False, y_at_n2[s][:, t, :], y_rows[t], n2_sb, c0, n, scale=0.5)
-                fetch(t < 2, y_at_n1[s][:, t, :], y_rows[t], n1_sb, c0, n)
-            if s == 0:
-                dst, src = dealt_views(w2_grouped, w2_raw, 0, P)
-                nc.vector.tensor_copy(dst, src)
-                quantize(w2_words, w2_scales, w2_grouped[:], 0, S)
-        res_sb = sb("res_sb", [P, PACK, S], F32, tag="staged")
+        z_rows = [sb(f"z_rows{c0}", [P, PACK, n], F32) for c0, n in SLICES]
+        half_y_at_n2 = [sb(f"half_y_at_n2_{c0}", [P, PACK, n], F32) for c0, n in SLICES]
+        for pair in range(2):
+            deal_pair(True, w2_grouped[:, 2 * S * pair : 2 * S * (pair + 1)], w2_raw, pair)
+        quantize(w2_words, w2_scales, w2_grouped, 0, S)
+        res_sb = shared.tile([P, PACK, S], F32, name="res_sb", offset=S, align_bytes=64)
         nc.sync.dma_start(res_sb[:], res.rearrange("(p t) j -> p t j", t=PACK))
-        for s, (c0, n) in enumerate(SLICES):
+
+        def mix(s):
+            c0, n = SLICES[s]
+            for t in range(PACK):
+                nc.scalar.activation(half_y_at_n2[s][:, t, :], looked_up(y_rows[t], n2_sb, c0, n), COPY, scale=0.5)
+                nc.vector.tensor_tensor(
+                    z_rows[s][:, t, :], looked_up(y_rows[t], n1_sb, c0, n), half_y_at_n2[s][:, t, :], ALU.add
+                )
+
+        def second_product(s):
+            c0, n = SLICES[s]
             z_grouped = sb(f"z_grouped{c0}", [P, PACK * n], BF16)
-            nc.vector.tensor_tensor(woven(z_grouped, 2), planar(y_at_n1[s], 2), planar(y_at_n2[s], 2), ALU.add)
-            quantize(z_words, z_scales, z_grouped[:], c0, n)
+            copy(s != Z_SLICE_ON_SCALAR, woven(z_grouped), planar(z_rows[s]))
+            quantize(z_words, z_scales, z_grouped, c0, n)
             b, o = divmod(c0, HALF)
             for t in range(PACK):
-                product(h_bank[b][t // 2][:, t % 2, o : o + n], w2_words, w2_scales, t, z_words, z_scales, c0, n)
+                product(h_bank[b][t % 2][:, t // 2, o : o + n], w2_words, w2_scales, t, z_words, z_scales, c0, n)
+
+        for step in range(len(SLICES) + 1):
+            if step <= LAST:
+                mix(step)
+            if step >= 1:
+                second_product(step - 1)
+
         for t in range(PACK):
-            nc.scalar.activation(h_rows[t][:, 0:HALF], h_bank[0][t // 2][:, t % 2, :], COPY)
+            copy(False, h_rows[t][:, 0:HALF], h_bank[0][t % 2][:, t // 2, :])
         w3_word_dealt = sb("w3_word_dealt", [P, S], U32)
         w3_scale_dealt = sb("w3_scale_dealt", [P, S], U8)
         nc.scalar.copy(
             w3_word_dealt[:].rearrange("p (t m) -> p m t", t=PACK), w3_word_raw[:].rearrange("p (m t) -> p m t", t=PACK)
         )
         nc.vector.tensor_copy(
-            w3_scale_dealt[:].rearrange("p (t m) -> p m t", t=PACK), w3_scale_raw[:].rearrange("p (m t) -> p m t", t=PACK)
+            w3_scale_dealt[:].rearrange("p (t m) -> p t m", t=PACK), w3_scale_raw[:].rearrange("p (m t) -> p t m", t=PACK)
         )
         for t in range(PACK):
-            if t < 2:
-                nc.scalar.activation(h_rows[t][:, HALF:S], h_bank[1][t // 2][:, t % 2, :], COPY)
-            else:
-                nc.vector.tensor_copy(h_rows[t][:, HALF:S], h_bank[1][t // 2][:, t % 2, :])
+            copy(t % 2 == 1, h_rows[t][:, HALF:S], h_bank[1][t % 2][:, t // 2, :])
 
         z2_words = sb("z2_words", [P, S], U32)
         z2_scales = sb("z2_scales", [P, S], U8)
         out_words = sb("out_words", [P, S], U32)
         out_scales = sb("out_scales", [P, S], U8)
         out_rows = out_0.rearrange("(p t) j -> p t j", t=PACK)
-        out_word_rows = out_1[0].rearrange("p n t -> p (n t)").bitcast(I32)
-        out_tags = (("y00", "y01"), ("h00",), ("h01",))
+        out_bank_tags = (("y00", "y01"), ("h00",), ("h01",))
         result = [sb(f"result{c0}", [P, PACK, n], F32) for c0, n in SLICES]
 
         def envelope(s):
@@ -192,50 +196,44 @@ def tile_picked_upenv_none_po_kernel(
             larger = sb(f"larger{c0}", [P, PACK, n], F32)
             smaller = sb(f"smaller{c0}", [P, PACK, n], F32)
             for u in range(2):
-                pair = slice(2 * u, 2 * u + 2)
-                for t in (2 * u, 2 * u + 1):
-                    fetch(s == 0 and t >= 1, h_at_n1[:, t, :], h_rows[t], n1_sb, c0, n)
-                for t in (2 * u, 2 * u + 1):
-                    fetch(False, h_at_n2[:, t, :], h_rows[t], n2_sb, c0, n)
+                for e in range(2):
+                    on_vector = s == 0 and 2 * u + e >= PACK - H_GATHERS_ON_VECTOR
+                    copy(on_vector, h_at_n1[:, u + 2 * e, :], looked_up(h_rows[u + 2 * e], n1_sb, c0, n))
+                for e in range(2):
+                    copy(False, h_at_n2[:, u + 2 * e, :], looked_up(h_rows[u + 2 * e], n2_sb, c0, n))
             for u in range(2):
-                pair = slice(2 * u, 2 * u + 2)
-                nc.vector.tensor_tensor(larger[:, pair, :], h_bank[b][u][:, :, o : o + n], h_at_n1[:, pair, :], ALU.max)
-                nc.vector.tensor_tensor(smaller[:, pair, :], y_bank[b][u][:, :, o : o + n], h_at_n2[:, pair, :], ALU.min)
+                tiles = slice(u, PACK, 2)
+                nc.vector.tensor_tensor(larger[:, tiles, :], h_bank[b][u][:, :, o : o + n], h_at_n1[:, tiles, :], ALU.max)
+                nc.vector.tensor_tensor(smaller[:, tiles, :], y_bank[b][u][:, :, o : o + n], h_at_n2[:, tiles, :], ALU.min)
             z2_grouped = sb(f"z2_grouped{c0}", [P, PACK * n], BF16)
-            nc.vector.tensor_tensor(woven(z2_grouped, 2), planar(larger, 2), planar(smaller, 2), ALU.subtract)
-            quantize(z2_words, z2_scales, z2_grouped[:], c0, n)
+            nc.vector.tensor_tensor(woven(z2_grouped), planar(larger), planar(smaller), ALU.subtract)
+            quantize(z2_words, z2_scales, z2_grouped, c0, n)
 
         def third_product(s):
             c0, n = SLICES[s]
-            per_bank = PACK // len(out_tags[s])
-            for u, tag in enumerate(out_tags[s]):
-                acc = bank(tag, [P, per_bank, n], f"out_bank{c0}_{u}")
+            per_bank = PACK // len(out_bank_tags[s])
+            for u, tag in enumerate(out_bank_tags[s]):
+                acc = bank(f"out_bank{c0}_{u}", [P, per_bank, n], tag)
                 for e in range(per_bank):
                     product(acc[:, e, :], w3_word_dealt, w3_scale_dealt, per_bank * u + e, z2_words, z2_scales, c0, n)
-                rows = slice(per_bank * u, per_bank * (u + 1))
-                nc.vector.tensor_tensor(result[s][:, rows, :], acc[:], res_sb[:, rows, c0 : c0 + n], ALU.add)
+                tiles = slice(per_bank * u, per_bank * (u + 1))
+                nc.vector.tensor_tensor(result[s][:, tiles, :], acc[:], res_sb[:, tiles, c0 : c0 + n], ALU.add)
             nc.sync.dma_start(out_rows[:, :, c0 : c0 + n], result[s][:])
 
-        def hand_on(s, on_vector):
+        def hand_on(s):
             c0, n = SLICES[s]
             out_grouped = sb(f"out_grouped{c0}", [P, PACK * n], BF16)
-            if on_vector:
-                nc.vector.tensor_copy(woven(out_grouped, 4), planar(result[s], 4))
-            else:
-                nc.scalar.activation(woven(out_grouped, 4), planar(result[s], 4), COPY)
-            quantize(out_words, out_scales, out_grouped[:], c0, n)
-            nc.sync.dma_start(out_word_rows[:, c0 : c0 + n], out_words[:, c0 : c0 + n].bitcast(I32))
+            copy(s == LAST, woven(out_grouped), planar(result[s]))
+            quantize(out_words, out_scales, out_grouped, c0, n)
+            nc.sync.dma_start(word_rows(out_1)[:, c0 : c0 + n], out_words[:, c0 : c0 + n].bitcast(I32))
 
-        envelope(0)
-        third_product(0)
-        envelope(1)
-        third_product(1)
-        envelope(2)
-        hand_on(0, False)
-        hand_on(1, False)
-        third_product(2)
-        hand_on(2, True)
-        for q in range(4):
+        stages = (envelope, third_product, hand_on)
+        for step in range(len(SLICES) + len(stages) - 1):
+            for lag, stage in enumerate(stages):
+                if 0 <= step - lag <= LAST:
+                    stage(step - lag)
+
+        for q in range(QUADRANTS):
             queue = nc.scalar if q % 2 else nc.sync
             queue.dma_start(
                 out_2[0, 4 * q : 4 * q + 4, :].bitcast(I32), out_scales[32 * q : 32 * q + 4, :].bitcast(I32)

from contextlib import ExitStack

import concourse.mybir as mybir

F32 = mybir.dt.float32
BF16 = mybir.dt.bfloat16
I32 = mybir.dt.int32
U32 = mybir.dt.uint32
U16 = mybir.dt.uint16
U8 = mybir.dt.uint8
FP8X4 = mybir.dt.float8_e4m3fn_x4
ALU = mybir.AluOpType
COPY = mybir.ActivationFunctionType.Copy

P = 128
PACK = 4
T = 2048
S = 512
HALF = S // 2
QUADRANTS = 4
PER_LIST_COLUMN = 16
WEAVE_RUN = 4
FLOPS = 3 * 2 * S * S * S

SLICES = ((0, 256), (256, 128), (384, 128))
LAST = len(SLICES) - 1
Y_TILES_SHARED = 2
Z_SLICE_ON_SCALAR = 1
H_GATHERS_ON_VECTOR = 3


def tile_picked_upenv_none_po_kernel(
    tc, x_words, x_scales, w1, w2, w3_words, w3_scales, res, offs, n1, n2, out_0, out_1, out_2
):
    nc = tc.nc
    with ExitStack() as ctx:
        keep = ctx.enter_context(tc.tile_pool(name="keep", bufs=1))
        shared = ctx.enter_context(tc.tile_pool(name="shared", bufs=1))
        psum = ctx.enter_context(tc.psum_pool(name="psum", bufs=1))

        def sb(name, shape, dtype, tag=None):
            return keep.tile(shape, dtype, name=name, tag=tag or name, align_bytes=64)

        def bank(name, shape, tag):
            return psum.tile(shape, F32, name=name, tag=tag)

        def copy(on_vector, dst, src):
            if on_vector:
                nc.vector.tensor_copy(dst, src)
            else:
                nc.scalar.activation(dst, src, COPY)

        def word_rows(packed):
            return packed[0].rearrange("p n t -> p (n t)").bitcast(I32)

        def load_scale_rows(queue, tile, scales):
            nc.gpsimd.memset(tile[:].bitcast(I32), 0)
            for q in range(QUADRANTS):
                queue.dma_start(tile[32 * q : 32 * q + 4, :].bitcast(I32), scales[0, 4 * q : 4 * q + 4, :].bitcast(I32))

        def deal_pair(on_vector, grouped, raw, pair):
            dst = grouped.rearrange("p (t m j) -> p m j t", t=2, j=PACK)
            src = raw[:].rearrange("p j (m t) -> p m j t", t=PACK)[:, :, :, 2 * pair : 2 * pair + 2]
            copy(on_vector, dst, src)

        def woven(grouped):
            return grouped[:].rearrange("p (c i t) -> p c t i", i=WEAVE_RUN, t=PACK)

        def planar(row_tiles):
            return row_tiles[:].rearrange("p t (c i) -> p c t i", i=WEAVE_RUN)

        def quantize(words, scales, grouped, c0, n):
            nc.vector.quantize_mx(
                out=words[:, c0 : c0 + n].bitcast(FP8X4), scales=scales[:, c0 : c0 + n], in_=grouped[:]
            )

        def product(out, w_words, w_scales, t, a_words, a_scales, c0, n):
            nc.tensor.matmul_mx(
                out=out,
                lhsT=w_words[:, P * t : P * (t + 1)].bitcast(FP8X4),
                lhsT_scale=w_scales[:, P * t : P * (t + 1)],
                rhs=a_words[:, c0 : c0 + n].bitcast(FP8X4),
                rhs_scale=a_scales[:, c0 : c0 + n],
                start=True,
                stop=True,
            )

        def looked_up(rows, index, c0, n):
            return rows[:].indirect(index[:, c0 // PER_LIST_COLUMN : (c0 + n) // PER_LIST_COLUMN])

        offs_sb = keep.tile([P, S // PER_LIST_COLUMN], U16, name="offs_sb")
        n1_sb = keep.tile([P, S // PER_LIST_COLUMN], U16, name="n1_sb")
        n2_sb = keep.tile([P, S // PER_LIST_COLUMN], U16, name="n2_sb")
        x_word_table = shared.tile([P, T], U32, name="x_word_table", offset=0, align_bytes=64)
        x_scale_table = sb("x_scale_table", [P, T], U8)
        w1_raw = sb("w1_raw", [P, PACK, S], F32, tag="w1_raw_then_w3_words")
        nc.sync.dma_start(offs_sb[:], offs)
        load_scale_rows(nc.scalar, x_scale_table, x_scales)
        nc.sync.dma_start(x_word_table[:].bitcast(I32), word_rows(x_words))
        nc.sync.dma_start(w1_raw[:], w1.rearrange("(p j) c -> p j c", j=PACK))
        nc.sync.dma_start(n1_sb[:], n1)
        nc.sync.dma_start(n2_sb[:], n2)

        x_word_pick = sb("x_word_pick", [P, S], U32)
        nc.vector.tensor_copy(x_word_pick[:], x_word_table[:].indirect(offs_sb[:]))
        x_scale_pick = shared.tile([P, S], U8, name="x_scale_pick", offset=0, align_bytes=64)
        nc.vector.tensor_copy(x_scale_pick[:], x_scale_table[:].indirect(offs_sb[:]))
        w2_raw = shared.tile([P, PACK, S], F32, name="w2_raw", offset=S, align_bytes=64)
        nc.sync.dma_start(w2_raw[:], w2.rearrange("(p j) c -> p j c", j=PACK))

        w1_words = sb("w1_words", [P, S], U32)
        w1_scales = sb("w1_scales", [P, S], U8)
        w1_grouped = [sb(f"w1_grouped{pair}", [P, 2 * S], BF16) for pair in range(2)]
        for pair in range(2):
            deal_pair(pair == 0, w1_grouped[pair][:], w1_raw, pair)
            quantize(w1_words, w1_scales, w1_grouped[pair], HALF * pair, HALF)
        w3_word_raw = sb("w3_word_raw", [P, S], U32, tag="w1_raw_then_w3_words")
        nc.sync.dma_start(w3_word_raw[:].bitcast(I32), word_rows(w3_words))
        w3_scale_raw = sb("w3_scale_raw", [P, S], U8, tag="w1_grouped0")
        load_scale_rows(nc.sync, w3_scale_raw, w3_scales)

        y_bank = [[bank(f"y_bank{b}{u}", [P, 2, HALF], f"y{b}{u}") for u in range(2)] for b in range(2)]
        h_bank = [[bank(f"h_bank{b}{u}", [P, 2, HALF], f"h{b}{u}") for u in range(2)] for b in range(2)]
        y_rows = [sb(f"y_rows{t}", [P, S], F32) for t in range(PACK)]
        h_rows = [sb(f"h_rows{t}", [P, S], F32) for t in range(PACK)]

        for t in range(PACK):
            for b in range(2):
                product(y_bank[b][t % 2][:, t // 2, :], w1_words, w1_scales, t, x_word_pick, x_scale_pick, HALF * b, HALF)
            for b in range(2):
                on_vector = b == 1 and t < Y_TILES_SHARED
                copy(on_vector, y_rows[t][:, HALF * b : HALF * (b + 1)], y_bank[b][t % 2][:, t // 2, :])

        w2_grouped = sb("w2_grouped", [P, PACK * S], BF16)
        w2_words = sb("w2_words", [P, S], U32)
        w2_scales = sb("w2_scales", [P, S], U8)
        z_words = sb("z_words", [P, S], U32)
        z_scales = sb("z_scales", [P, S], U8)
        z_rows = [sb(f"z_rows{c0}", [P, PACK, n], F32) for c0, n in SLICES]
        half_y_at_n2 = [sb(f"half_y_at_n2_{c0}", [P, PACK, n], F32) for c0, n in SLICES]
        for pair in range(2):
            deal_pair(True, w2_grouped[:, 2 * S * pair : 2 * S * (pair + 1)], w2_raw, pair)
        quantize(w2_words, w2_scales, w2_grouped, 0, S)
        res_sb = shared.tile([P, PACK, S], F32, name="res_sb", offset=S, align_bytes=64)
        nc.sync.dma_start(res_sb[:], res.rearrange("(p t) j -> p t j", t=PACK))

        def mix(s):
            c0, n = SLICES[s]
            for t in range(PACK):
                nc.scalar.activation(half_y_at_n2[s][:, t, :], looked_up(y_rows[t], n2_sb, c0, n), COPY, scale=0.5)
                nc.vector.tensor_tensor(
                    z_rows[s][:, t, :], looked_up(y_rows[t], n1_sb, c0, n), half_y_at_n2[s][:, t, :], ALU.add
                )

        def second_product(s):
            c0, n = SLICES[s]
            z_grouped = sb(f"z_grouped{c0}", [P, PACK * n], BF16)
            copy(s != Z_SLICE_ON_SCALAR, woven(z_grouped), planar(z_rows[s]))
            quantize(z_words, z_scales, z_grouped, c0, n)
            b, o = divmod(c0, HALF)
            for t in range(PACK):
                product(h_bank[b][t % 2][:, t // 2, o : o + n], w2_words, w2_scales, t, z_words, z_scales, c0, n)

        for step in range(len(SLICES) + 1):
            if step <= LAST:
                mix(step)
            if step >= 1:
                second_product(step - 1)

        for t in range(PACK):
            copy(False, h_rows[t][:, 0:HALF], h_bank[0][t % 2][:, t // 2, :])
        w3_word_dealt = sb("w3_word_dealt", [P, S], U32)
        w3_scale_dealt = sb("w3_scale_dealt", [P, S], U8)
        nc.scalar.copy(
            w3_word_dealt[:].rearrange("p (t m) -> p m t", t=PACK), w3_word_raw[:].rearrange("p (m t) -> p m t", t=PACK)
        )
        nc.vector.tensor_copy(
            w3_scale_dealt[:].rearrange("p (t m) -> p t m", t=PACK), w3_scale_raw[:].rearrange("p (m t) -> p t m", t=PACK)
        )
        for t in range(PACK):
            copy(t % 2 == 1, h_rows[t][:, HALF:S], h_bank[1][t % 2][:, t // 2, :])

        z2_words = sb("z2_words", [P, S], U32)
        z2_scales = sb("z2_scales", [P, S], U8)
        out_words = sb("out_words", [P, S], U32)
        out_scales = sb("out_scales", [P, S], U8)
        out_rows = out_0.rearrange("(p t) j -> p t j", t=PACK)
        out_bank_tags = (("y00", "y01"), ("h00",), ("h01",))
        result = [sb(f"result{c0}", [P, PACK, n], F32) for c0, n in SLICES]

        def envelope(s):
            c0, n = SLICES[s]
            b, o = divmod(c0, HALF)
            h_at_n1 = sb(f"h_at_n1_{c0}", [P, PACK, n], F32)
            h_at_n2 = sb(f"h_at_n2_{c0}", [P, PACK, n], F32)
            larger = sb(f"larger{c0}", [P, PACK, n], F32)
            smaller = sb(f"smaller{c0}", [P, PACK, n], F32)
            for u in range(2):
                for e in range(2):
                    on_vector = s == 0 and 2 * u + e >= PACK - H_GATHERS_ON_VECTOR
                    copy(on_vector, h_at_n1[:, u + 2 * e, :], looked_up(h_rows[u + 2 * e], n1_sb, c0, n))
                for e in range(2):
                    copy(False, h_at_n2[:, u + 2 * e, :], looked_up(h_rows[u + 2 * e], n2_sb, c0, n))
            for u in range(2):
                tiles = slice(u, PACK, 2)
                nc.vector.tensor_tensor(larger[:, tiles, :], h_bank[b][u][:, :, o : o + n], h_at_n1[:, tiles, :], ALU.max)
                nc.vector.tensor_tensor(smaller[:, tiles, :], y_bank[b][u][:, :, o : o + n], h_at_n2[:, tiles, :], ALU.min)
            z2_grouped = sb(f"z2_grouped{c0}", [P, PACK * n], BF16)
            nc.vector.tensor_tensor(woven(z2_grouped), planar(larger), planar(smaller), ALU.subtract)
            quantize(z2_words, z2_scales, z2_grouped, c0, n)

        def third_product(s):
            c0, n = SLICES[s]
            per_bank = PACK // len(out_bank_tags[s])
            for u, tag in enumerate(out_bank_tags[s]):
                acc = bank(f"out_bank{c0}_{u}", [P, per_bank, n], tag)
                for e in range(per_bank):
                    product(acc[:, e, :], w3_word_dealt, w3_scale_dealt, per_bank * u + e, z2_words, z2_scales, c0, n)
                tiles = slice(per_bank * u, per_bank * (u + 1))
                nc.vector.tensor_tensor(result[s][:, tiles, :], acc[:], res_sb[:, tiles, c0 : c0 + n], ALU.add)
            nc.sync.dma_start(out_rows[:, :, c0 : c0 + n], result[s][:])

        def hand_on(s):
            c0, n = SLICES[s]
            out_grouped = sb(f"out_grouped{c0}", [P, PACK * n], BF16)
            copy(s == LAST, woven(out_grouped), planar(result[s]))
            quantize(out_words, out_scales, out_grouped, c0, n)
            nc.sync.dma_start(word_rows(out_1)[:, c0 : c0 + n], out_words[:, c0 : c0 + n].bitcast(I32))

        stages = (envelope, third_product, hand_on)
        for step in range(len(SLICES) + len(stages) - 1):
            for lag, stage in enumerate(stages):
                if 0 <= step - lag <= LAST:
                    stage(step - lag)

        for q in range(QUADRANTS):
            queue = nc.scalar if q % 2 else nc.sync
            queue.dma_start(
                out_2[0, 4 * q : 4 * q + 4, :].bitcast(I32), out_scales[32 * q : 32 * q + 4, :].bitcast(I32)
            )
